import numpy as np, ml_dtypes
CORES = [211,219,227,235,243,251,83,91,99,107,115,123]
N = 12
VB, TK = 2, 64
def setup_inputs(rng):
    h = (rng.standard_normal((128, TK), dtype=np.float32) / 8).astype(ml_dtypes.bfloat16)
    return {"h": np.broadcast_to(h, (N, 128, TK)).copy(), "w": rng.standard_normal((N, 128, VB * 128), dtype=np.float32).astype(ml_dtypes.bfloat16)}
def setup_inputs_big(rng):
    d = setup_inputs(rng)
    for k in ("h", "w"): d[k] = (d[k].astype(np.float32) * 1024.0).astype(d[k].dtype)
    return d
def setup_inputs_small(rng):
    d = setup_inputs(rng)
    for k in ("h", "w"): d[k] = (d[k].astype(np.float32) * (1 / 1024.0)).astype(d[k].dtype)
    return d
def setup_inputs_apart(rng):
    d = setup_inputs(rng)
    f = (10.0 ** rng.permutation(np.linspace(-1.5, 1.5, N))).astype(np.float32).reshape(N, 1, 1)
    for k in ("w",): d[k] = (d[k].astype(np.float32) * f).astype(d[k].dtype)
    return d
def setup_inputs_neg(rng):
    d = setup_inputs(rng)
    d["h"] = (np.abs(d["h"].astype(np.float32)) * 1048576.0).astype(d["h"].dtype); d["w"] = (-np.abs(d["w"].astype(np.float32))).astype(d["w"].dtype)
    return d
def reference(h, w):
    H, W = h.astype(np.float64), w.astype(np.float64)
    Z = np.concatenate([W[r].T @ H[r] for r in range(N)], axis=0)
    m = Z.max(axis=0)
    s = np.maximum(Z - 0.5 * m, 0.0).sum(axis=0)
    return {"m": np.broadcast_to(m.astype(np.float32), (N, 1, TK)), "s": np.broadcast_to(s.astype(np.float32), (N, 1, TK))}

@@ -1,0 +1,208 @@
+from concourse.bass import DstId, RemoteDMATransfer
+from concourse.mybir import AluOpType
+
+N, TK = 12, 64
+R1_DRAM = True
+R2_DRAM = True
+NENG = 4
+
+SCRATCH = {
+    "wS": ("sbuf", [128, 256], "bfloat16"),
+    "hS": ("sbuf", [128, TK], "bfloat16"),
+    "zA": ("psum", [128, 512], "float32"),
+    "zB0": ("psum", [128, 512], "float32"),
+    "zB1": ("psum", [128, 512], "float32"),
+    "pT1": ("psum", [128, 512], "float32"),
+    "pT2": ("psum", [128, 512], "float32"),
+    "pS": ("psum", [128, 512], "float32"),
+    "pF": ("psum", [128, 512], "float32"),
+    "tr": ("sbuf", [128, 448], "float32"),
+    "ones": ("sbuf", [128, 4], "float32"),
+    "nh": ("sbuf", [128, 128], "float32"),
+    "zeros": ("sbuf", [128, TK], "float32"),
+    "idA": ("sbuf", [128, TK + 1], "float32"),
+    "idD": ("dram", [1, TK * (TK + 1)], "float32"),
+    "idI": ("sbuf", [128, TK], "float32"),
+    "R": ("sbuf", [128, 128], "float32"),
+    "U1": ("sbuf", [128, TK], "float32"),
+    "U2": ("sbuf", [128, TK], "float32"),
+    "mrow": ("sbuf", [128, TK], "float32"),
+    "srow": ("sbuf", [128, 2 * TK], "float32"),
+    "fin": ("sbuf", [128, TK], "float32"),
+    "land1": ("dram", [N, 128, 1], "float32"),
+    "land2": ("dram", [N, 128, 1], "float32"),
+    "l1s": ("sbuf", [128, 4 * N], "float32"),
+    "l2s": ("sbuf", [128, 4 * N], "float32"),
+}
+SEMAPHORES = ["ld", "ini", "ida", "idd", "vq", "pza", "pt1", "pt2", "pb0", "pb1", "ps", "pf",
+              "st1", "st2", "u1", "u2", "arr1", "arr2", "sent", "outm", "outs"]
+
+
+def rank_program(g, core, T, topo):
+    rank = T.rank_of(core)
+    if rank is None:
+        return
+    S = T.sem
+    V, PE, SY, SC = g.vector, g.tensor, g.sync, g.scalar
+    MAX, ADD = AluOpType.max, AluOpType.add
+    tr = T.tr
+
+    peers = [c for c in T.cores if c != core]
+    peers.sort(key=lambda d: 1 if (topo.mates(core, d) or topo.same_plane(core, d)) else 0)
+    common = topo.mask(core, peers[0])
+    for d in peers:
+        common &= topo.mask(core, d)
+    bits = [1 << b for b in range(common.bit_length()) if (common >> b) & 1]
+
+    def dst_id(d):
+        rid, pid = topo.addr(d, core)
+        return DstId(rid=rid, pnc=pid)
+
+    def send(ap, sem, masks):
+        k = len(masks)
+        trs = []
+        for i in range(k):
+            ds = peers[i::k]
+            trs.append(RemoteDMATransfer(dst_ids=[dst_id(d) for d in ds], dma_engine_mask=masks[i], remote_sem=sem,
+                                         srcs=[ap], dsts=[ap for _ in ds], alu_op=0))
+        g.remote_dma_fused(trs, local_sem=S.sent)
+
+    one_each = bits[::len(bits) // NENG][:NENG]
+    all_bits = [sum(bits)]
+    sent = 0
+
+    vc = [0]
+
+    def vdo(ins):
+        ins.then_inc(S.vq, 1)
+        vc[0] += 1
+        V.wait_ge(S.vq, vc[0])
+        return vc[0]
+
+    def fold12(op, a, b, base, out):
+        vdo(V.tensor_tensor(tr[0:64, base:base + 6], a, b, op))
+        vdo(V.tensor_tensor(tr[0:64, base + 8:base + 11], tr[0:64, base:base + 3], tr[0:64, base + 3:base + 6], op))
+        vdo(V.tensor_tensor(tr[0:64, base + 12:base + 13], tr[0:64, base + 8:base + 9], tr[0:64, base + 9:base + 10], op))
+        return vdo(V.tensor_tensor(out, tr[0:64, base + 12:base + 13], tr[0:64, base + 10:base + 11], op))
+
+    SY.dma_start(T.wS[:, :], T.w[:, :]).then_inc(S.ld, 16)
+    SC.dma_start(T.hS[:, :], T.h[:, :]).then_inc(S.ld, 16)
+    fills = [(T.idA[0:64, 1:TK + 1], 0.0), (T.idA[0:64, 0:1], 1.0), (T.ones[:, 0:4], 1.0),
+             (T.nh[0:1, :], -0.5), (T.zeros[:, :], 0.0)]
+    own = slice(4 * rank, 4 * rank + 1)
+    if R1_DRAM:
+        fills.append((tr[64:128, 384:388], 0.0))
+    else:
+        fills.append((T.l1s[64:128, 4 * rank:4 * rank + 4], 0.0))
+    if R2_DRAM:
+        fills.append((T.srow[0:1, TK:2 * TK], 0.0))
+    else:
+        fills.append((T.l2s[64:128, 4 * rank:4 * rank + 4], 0.0))
+    for ap, c in fills:
+        V.memset(ap, c).then_inc(S.ini, 1)
+    nini = len(fills)
+    V.wait_ge(S.ini, nini)
+    SY.wait_ge(S.ini, nini)
+    SC.wait_ge(S.ini, nini)
+    SC.dma_start(T.idD[0, :], T.idA[0:TK, 0:TK + 1]).then_inc(S.ida, 16)
+    SC.wait_ge(S.ida, 16)
+    SC.dma_start(T.idI[0:TK, 0:TK], T.idD[0, 0:TK * TK]).then_inc(S.idd, 16)
+
+    PE.wait_ge(S.ld, 32)
+    PE.matmul(T.zA[0:64, 0:256], T.hS[:, :], T.wS[:, :], True, True).then_inc(S.pza, 1)
+    PE.matmul(T.zB0[:, 0:64], T.wS[:, 0:128], T.hS[:, :], True, False)
+    PE.matmul(T.zB1[:, 0:64], T.wS[:, 128:256], T.hS[:, :], True, False)
+
+    V.wait_ge(S.pza, 1)
+    vdo(V.tensor_copy(tr[0:64, 0:128], T.zA[0:64, 0:128]))
+    vdo(V.tensor_tensor(tr[0:64, 128:256], T.zA[0:64, 128:256], tr[0:64, 0:128], MAX))
+    lo, w, nxt = 128, 128, 256
+    while w > 1:
+        hw = w // 2
+        dest = tr[0:64, nxt:nxt + hw]
+        if hw == 1 and not R1_DRAM:
+            dest = T.l1s[0:64, own]
+        n_col = vdo(V.tensor_tensor(dest, tr[0:64, lo:lo + hw], tr[0:64, lo + hw:lo + w], MAX))
+        lo, w, nxt = nxt, hw, nxt + max(hw, 4)
+    mcol = tr[0:64, 416:417]
+
+    if R1_DRAM:
+        SY.wait_ge(S.vq, n_col)
+        SY.dma_start(T.land1[rank, :, 0], tr[:, lo:lo + 1]).then_inc(S.st1, 16)
+        g.wait_ge(S.st1, 16)
+        send(T.land1[rank], S.arr1, one_each)
+        sent += NENG
+        SY.wait_ge(S.st1, 16)
+        SY.wait_ge(S.arr1, N - 1)
+        SY.dma_start(T.U1[0:N, 0:64], T.land1[:, 0:64, 0]).then_inc(S.u1, 16)
+        PE.wait_ge(S.idd, 16)
+        PE.wait_ge(S.u1, 16)
+        PE.matmul(T.pT1[0:64, 0:N], T.U1[0:N, 0:64], T.idI[0:N, 0:N], True, True).then_inc(S.pt1, 1)
+        V.wait_ge(S.pt1, 1)
+        vdo(V.tensor_copy(tr[0:64, 392:398], T.pT1[0:64, 0:6]))
+        n_mcol = fold12(MAX, T.pT1[0:64, 6:12], tr[0:64, 392:398], 400, mcol)
+    else:
+        g.wait_ge(S.ini, nini)
+        g.wait_ge(S.vq, n_col)
+        send(T.l1s[:, own], S.arr1, all_bits)
+        sent += len(bits)
+        V.wait_ge(S.arr1, (N - 1) * len(bits))
+        n_mcol = fold12(MAX, T.l1s[0:64, 0:24:4], T.l1s[0:64, 24:48:4], 400, mcol)
+        PE.wait_ge(S.idd, 16)
+
+    PE.wait_ge(S.vq, n_mcol)
+    PE.matmul(T.pT2[0:1, 0:64], mcol, T.idI[0:64, 0:64], True, True).then_inc(S.pt2, 1)
+    V.wait_ge(S.pt2, 1)
+    n_mrow = vdo(V.tensor_copy(T.mrow[0:1, :], T.pT2[0:1, 0:64]))
+    SC.wait_ge(S.vq, n_mrow)
+    SC.dma_start(T.m[:, :], T.mrow[0:1, :]).then_inc(S.outm, 16)
+
+    PE.wait_ge(S.ini, nini)
+    PE.wait_ge(S.vq, n_mrow)
+    PE.matmul(T.zB0[:, 0:64], T.nh[0:1, :], T.mrow[0:1, :], False, True).then_inc(S.pb0, 1)
+    PE.matmul(T.zB1[:, 0:64], T.nh[0:1, :], T.mrow[0:1, :], False, True).then_inc(S.pb1, 1)
+    V.wait_ge(S.pb0, 1)
+    n_r0 = vdo(V.tensor_tensor(T.R[:, 0:64], T.zB0[:, 0:64], T.zeros[:, :], MAX))
+    V.wait_ge(S.pb1, 1)
+    n_r1 = vdo(V.tensor_tensor(T.R[:, 64:128], T.zB1[:, 0:64], T.zeros[:, :], MAX))
+
+    if R2_DRAM:
+        PE.wait_ge(S.vq, n_r0)
+        PE.matmul(T.pS[0:1, 0:64], T.ones[:, 0:1], T.R[:, 0:64], True, False)
+        PE.wait_ge(S.vq, n_r1)
+        PE.matmul(T.pS[0:1, 0:64], T.ones[:, 0:1], T.R[:, 64:128], False, True).then_inc(S.ps, 1)
+        V.wait_ge(S.ps, 1)
+        n_s = vdo(V.tensor_copy(T.srow[0:1, 0:TK], T.pS[0:1, 0:64]))
+        SY.wait_ge(S.vq, n_s)
+        SY.dma_start(T.land2[rank, :, 0], T.srow[0:1, :]).then_inc(S.st2, 16)
+        g.wait_ge(S.st2, 16)
+        send(T.land2[rank], S.arr2, one_each)
+        sent += NENG
+        SY.wait_ge(S.st2, 16)
+        SY.wait_ge(S.arr2, N - 1)
+        SY.dma_start(T.U2[0:N, 0:64], T.land2[:, 0:64, 0]).then_inc(S.u2, 16)
+        PE.wait_ge(S.u2, 16)
+        PE.matmul(T.pF[0:1, 0:64], T.ones[0:N, 0:1], T.U2[0:N, 0:64], True, True).then_inc(S.pf, 1)
+        V.wait_ge(S.pf, 1)
+        n_f = vdo(V.tensor_copy(T.fin[0:1, :], T.pF[0:1, 0:64]))
+        SY.wait_ge(S.vq, n_f)
+        SY.dma_start(T.s[:, :], T.fin[0:1, :]).then_inc(S.outs, 16)
+    else:
+        PE.wait_ge(S.vq, n_r0)
+        PE.matmul(T.pS[0:64, 0:1], T.R[:, 0:64], T.ones[:, 0:1], True, False)
+        PE.wait_ge(S.vq, n_r1)
+        PE.matmul(T.pS[0:64, 0:1], T.R[:, 64:128], T.ones[:, 0:1], False, True).then_inc(S.ps, 1)
+        V.wait_ge(S.ps, 1)
+        n_s = vdo(V.tensor_copy(T.l2s[0:64, own], T.pS[0:64, 0:1]))
+        g.wait_ge(S.ini, nini)
+        g.wait_ge(S.vq, n_s)
+        send(T.l2s[:, own], S.arr2, all_bits)
+        sent += len(bits)
+        V.wait_ge(S.arr2, (N - 1) * len(bits))
+        n_f = fold12(ADD, T.l2s[0:64, 0:24:4], T.l2s[0:64, 24:48:4], 424, tr[0:64, 440:441])
+        SY.wait_ge(S.vq, n_f)
+        SY.dma_start(T.s[0, :], tr[0:64, 440:441]).then_inc(S.outs, 16)
+
+    SY.wait_ge(S.outs, 16)
+    SC.wait_ge(S.outm, 16)
+    g.wait_ge(S.sent, sent)

@@ -2,74 +2,83 @@ from concourse.bass import DstId, RemoteDMATransfer
 from concourse.mybir import AluOpType
 
 N, TK = 12, 64
-R1_DRAM = True
-R2_DRAM = True
+NCORES = 256
 NENG = 4
 
 SCRATCH = {
-    "wS": ("sbuf", [128, 256], "bfloat16"),
-    "hS": ("sbuf", [128, TK], "bfloat16"),
+    "wh": ("sbuf", [128, 448], "bfloat16"),
     "zA": ("psum", [128, 512], "float32"),
-    "zB0": ("psum", [128, 512], "float32"),
-    "zB1": ("psum", [128, 512], "float32"),
+    "zB": ("psum", [128, 512], "float32"),
     "pT1": ("psum", [128, 512], "float32"),
     "pT2": ("psum", [128, 512], "float32"),
     "pS": ("psum", [128, 512], "float32"),
     "pF": ("psum", [128, 512], "float32"),
-    "tr": ("sbuf", [128, 448], "float32"),
+    "tr": ("sbuf", [128, 256], "float32"),
     "ones": ("sbuf", [128, 4], "float32"),
     "nh": ("sbuf", [128, 128], "float32"),
     "zeros": ("sbuf", [128, TK], "float32"),
     "idA": ("sbuf", [128, TK + 1], "float32"),
     "idD": ("dram", [1, TK * (TK + 1)], "float32"),
     "idI": ("sbuf", [128, TK], "float32"),
-    "R": ("sbuf", [128, 128], "float32"),
+    "R": ("sbuf", [128, TK], "float32"),
     "U1": ("sbuf", [128, TK], "float32"),
     "U2": ("sbuf", [128, TK], "float32"),
     "mrow": ("sbuf", [128, TK], "float32"),
     "srow": ("sbuf", [128, 2 * TK], "float32"),
     "fin": ("sbuf", [128, TK], "float32"),
     "land1": ("dram", [N, 128, 1], "float32"),
-    "land2": ("dram", [N, 128, 1], "float32"),
-    "l1s": ("sbuf", [128, 4 * N], "float32"),
-    "l2s": ("sbuf", [128, 4 * N], "float32"),
+    "land2": ("dram", [2 * N, 128, 1], "float32"),
 }
-SEMAPHORES = ["ld", "ini", "ida", "idd", "vq", "pza", "pt1", "pt2", "pb0", "pb1", "ps", "pf",
+SEMAPHORES = ["ld", "ini", "ida", "idd", "idr", "whr", "vq", "pza", "pt1", "pt2", "pb", "ps", "pf",
               "st1", "st2", "u1", "u2", "arr1", "arr2", "sent", "outm", "outs"]
 
 
 def rank_program(g, core, T, topo):
-    rank = T.rank_of(core)
-    if rank is None:
+    ranks = list(T.cores)
+    helpers = []
+    for rk in ranks:
+        cand = [c for c in range(NCORES) if c != rk and topo.host(c) == topo.host(rk) and topo.chip(c) == topo.chip(rk)
+                and all(topo.may_write(c, d) for d in ranks)]
+        cand.sort(key=lambda c: 0 if topo.die(c) == topo.die(rk) else 1)
+        helpers.append(cand[0])
+    is_rank = core in ranks
+    if not is_rank and core not in helpers:
         return
+    r = ranks.index(core) if is_rank else helpers.index(core)
+    partner = helpers[r] if is_rank else ranks[r]
     S = T.sem
     V, PE, SY, SC = g.vector, g.tensor, g.sync, g.scalar
-    MAX, ADD = AluOpType.max, AluOpType.add
-    tr = T.tr
+    MAX = AluOpType.max
+    tr, wh = T.tr, T.wh
+    hS = wh[:, 320:384]
 
-    peers = [c for c in T.cores if c != core]
-    peers.sort(key=lambda d: 1 if (topo.mates(core, d) or topo.same_plane(core, d)) else 0)
-    common = topo.mask(core, peers[0])
-    for d in peers:
+    def far_first(ds):
+        return sorted(ds, key=lambda d: 0 if (topo.chip(d) != topo.chip(core) or topo.host(d) != topo.host(core))
+                      and not (topo.mates(core, d) or topo.same_plane(core, d)) else 1)
+
+    readers1 = far_first([d for d in ranks + helpers if d != core])
+    readers2 = far_first([d for d in ranks if d != core])
+    common = topo.mask(core, readers1[0])
+    for d in readers1:
         common &= topo.mask(core, d)
     bits = [1 << b for b in range(common.bit_length()) if (common >> b) & 1]
+    engines = bits[::len(bits) // NENG][:NENG]
 
     def dst_id(d):
         rid, pid = topo.addr(d, core)
         return DstId(rid=rid, pnc=pid)
 
-    def send(ap, sem, masks):
-        k = len(masks)
+    def send(ap, sem, readers):
         trs = []
-        for i in range(k):
-            ds = peers[i::k]
-            trs.append(RemoteDMATransfer(dst_ids=[dst_id(d) for d in ds], dma_engine_mask=masks[i], remote_sem=sem,
+        for i in range(NENG):
+            ds = readers[i::NENG]
+            trs.append(RemoteDMATransfer(dst_ids=[dst_id(d) for d in ds], dma_engine_mask=engines[i], remote_sem=sem,
                                          srcs=[ap], dsts=[ap for _ in ds], alu_op=0))
         g.remote_dma_fused(trs, local_sem=S.sent)
 
-    one_each = bits[::len(bits) // NENG][:NENG]
-    all_bits = [sum(bits)]
-    sent = 0
+    def hand(ap, sem):
+        g.remote_dma_fused([RemoteDMATransfer(dst_ids=[dst_id(partner)], dma_engine_mask=sum(engines), remote_sem=sem,
+                                              srcs=[ap], dsts=[ap], alu_op=0)], local_sem=S.sent)
 
     vc = [0]
 
@@ -79,130 +88,97 @@ def rank_program(g, core, T, topo):
         V.wait_ge(S.vq, vc[0])
         return vc[0]
 
-    def fold12(op, a, b, base, out):
-        vdo(V.tensor_tensor(tr[0:64, base:base + 6], a, b, op))
-        vdo(V.tensor_tensor(tr[0:64, base + 8:base + 11], tr[0:64, base:base + 3], tr[0:64, base + 3:base + 6], op))
-        vdo(V.tensor_tensor(tr[0:64, base + 12:base + 13], tr[0:64, base + 8:base + 9], tr[0:64, base + 9:base + 10], op))
-        return vdo(V.tensor_tensor(out, tr[0:64, base + 12:base + 13], tr[0:64, base + 10:base + 11], op))
-
-    SY.dma_start(T.wS[:, :], T.w[:, :]).then_inc(S.ld, 16)
-    SC.dma_start(T.hS[:, :], T.h[:, :]).then_inc(S.ld, 16)
-    fills = [(T.idA[0:64, 1:TK + 1], 0.0), (T.idA[0:64, 0:1], 1.0), (T.ones[:, 0:4], 1.0),
-             (T.nh[0:1, :], -0.5), (T.zeros[:, :], 0.0)]
-    own = slice(4 * rank, 4 * rank + 1)
-    if R1_DRAM:
-        fills.append((tr[64:128, 384:388], 0.0))
+    fills = [(T.ones[:, 0:4], 1.0), (T.nh[0:1, :], -0.5), (T.zeros[:, :], 0.0), (T.srow[0:1, TK:2 * TK], 0.0)]
+    if is_rank:
+        SY.dma_start(wh[:, 0:256], T.w[:, :]).then_inc(S.ld, 16)
+        SC.dma_start(hS, T.h[:, :]).then_inc(S.ld, 16)
+        fills = [(wh[:, 256:320], 0.0), (wh[:, 384:448], 0.0)] + fills
     else:
-        fills.append((T.l1s[64:128, 4 * rank:4 * rank + 4], 0.0))
-    if R2_DRAM:
-        fills.append((T.srow[0:1, TK:2 * TK], 0.0))
-    else:
-        fills.append((T.l2s[64:128, 4 * rank:4 * rank + 4], 0.0))
+        fills = [(T.idA[0:64, 1:TK + 1], 0.0), (T.idA[0:64, 0:1], 1.0), (T.idI[64:128, :], 0.0)] + fills
     for ap, c in fills:
         V.memset(ap, c).then_inc(S.ini, 1)
     nini = len(fills)
-    V.wait_ge(S.ini, nini)
-    SY.wait_ge(S.ini, nini)
-    SC.wait_ge(S.ini, nini)
-    SC.dma_start(T.idD[0, :], T.idA[0:TK, 0:TK + 1]).then_inc(S.ida, 16)
-    SC.wait_ge(S.ida, 16)
-    SC.dma_start(T.idI[0:TK, 0:TK], T.idD[0, 0:TK * TK]).then_inc(S.idd, 16)
+    for q in (V, SY, SC, PE, g):
+        q.wait_ge(S.ini, nini)
 
-    PE.wait_ge(S.ld, 32)
-    PE.matmul(T.zA[0:64, 0:256], T.hS[:, :], T.wS[:, :], True, True).then_inc(S.pza, 1)
-    PE.matmul(T.zB0[:, 0:64], T.wS[:, 0:128], T.hS[:, :], True, False)
-    PE.matmul(T.zB1[:, 0:64], T.wS[:, 128:256], T.hS[:, :], True, False)
-
-    V.wait_ge(S.pza, 1)
-    vdo(V.tensor_copy(tr[0:64, 0:128], T.zA[0:64, 0:128]))
-    vdo(V.tensor_tensor(tr[0:64, 128:256], T.zA[0:64, 128:256], tr[0:64, 0:128], MAX))
-    lo, w, nxt = 128, 128, 256
-    while w > 1:
-        hw = w // 2
-        dest = tr[0:64, nxt:nxt + hw]
-        if hw == 1 and not R1_DRAM:
-            dest = T.l1s[0:64, own]
-        n_col = vdo(V.tensor_tensor(dest, tr[0:64, lo:lo + hw], tr[0:64, lo + hw:lo + w], MAX))
-        lo, w, nxt = nxt, hw, nxt + max(hw, 4)
-    mcol = tr[0:64, 416:417]
-
-    if R1_DRAM:
+    if is_rank:
+        g.wait_ge(S.ld, 32)
+        hand(wh[:, 128:384], S.whr)
+        PE.wait_ge(S.ld, 32)
+        PE.matmul(T.zA[:, 0:128], wh[:, 320:448], wh[:, 0:128], True, False)
+        PE.matmul(T.zA[:, 0:128], wh[:, 256:384], wh[:, 128:256], False, True).then_inc(S.pza, 1)
+        PE.matmul(T.zB[:, 0:64], wh[:, 0:128], hS, True, False)
+        V.wait_ge(S.pza, 1)
+        vdo(V.tensor_copy(tr[:, 0:64], T.zA[:, 0:64]))
+        vdo(V.tensor_tensor(tr[:, 64:128], T.zA[:, 64:128], tr[:, 0:64], MAX))
+        lo, w, nxt = 64, 64, 128
+        while w > 1:
+            hw = w // 2
+            n_col = vdo(V.tensor_tensor(tr[:, nxt:nxt + hw], tr[:, lo:lo + hw], tr[:, lo + hw:lo + w], MAX))
+            lo, w, nxt = nxt, hw, nxt + max(hw, 4)
         SY.wait_ge(S.vq, n_col)
-        SY.dma_start(T.land1[rank, :, 0], tr[:, lo:lo + 1]).then_inc(S.st1, 16)
+        SY.dma_start(T.land1[r, :, 0], tr[:, lo:lo + 1]).then_inc(S.st1, 16)
         g.wait_ge(S.st1, 16)
-        send(T.land1[rank], S.arr1, one_each)
-        sent += NENG
+        send(T.land1[r], S.arr1, readers1)
         SY.wait_ge(S.st1, 16)
         SY.wait_ge(S.arr1, N - 1)
-        SY.dma_start(T.U1[0:N, 0:64], T.land1[:, 0:64, 0]).then_inc(S.u1, 16)
-        PE.wait_ge(S.idd, 16)
-        PE.wait_ge(S.u1, 16)
-        PE.matmul(T.pT1[0:64, 0:N], T.U1[0:N, 0:64], T.idI[0:N, 0:N], True, True).then_inc(S.pt1, 1)
-        V.wait_ge(S.pt1, 1)
-        vdo(V.tensor_copy(tr[0:64, 392:398], T.pT1[0:64, 0:6]))
-        n_mcol = fold12(MAX, T.pT1[0:64, 6:12], tr[0:64, 392:398], 400, mcol)
+        PE.wait_ge(S.idr, NENG)
     else:
-        g.wait_ge(S.ini, nini)
-        g.wait_ge(S.vq, n_col)
-        send(T.l1s[:, own], S.arr1, all_bits)
-        sent += len(bits)
-        V.wait_ge(S.arr1, (N - 1) * len(bits))
-        n_mcol = fold12(MAX, T.l1s[0:64, 0:24:4], T.l1s[0:64, 24:48:4], 400, mcol)
+        SC.dma_start(T.idD[0, :], T.idA[0:TK, 0:TK + 1]).then_inc(S.ida, 16)
+        SC.wait_ge(S.ida, 16)
+        SC.dma_start(T.idI[0:TK, 0:TK], T.idD[0, 0:TK * TK]).then_inc(S.idd, 16)
+        g.wait_ge(S.idd, 16)
+        hand(T.idI[:, :], S.idr)
+        PE.wait_ge(S.whr, NENG)
+        PE.matmul(T.zB[:, 0:64], wh[:, 128:256], hS, True, False)
+        SY.wait_ge(S.arr1, N)
         PE.wait_ge(S.idd, 16)
+
+    SY.dma_start(T.U1[0:2 * N, 0:64], T.land1[:, :, 0]).then_inc(S.u1, 16)
+    PE.wait_ge(S.u1, 16)
+    PE.matmul(T.pT1[0:64, 0:2 * N], T.U1[0:2 * N, 0:64], T.idI[0:2 * N, 0:2 * N], True, True).then_inc(S.pt1, 1)
+    V.wait_ge(S.pt1, 1)
+    vdo(V.tensor_copy(tr[0:64, 200:212], T.pT1[0:64, 0:12]))
+    vdo(V.tensor_tensor(tr[0:64, 212:224], T.pT1[0:64, 12:24], tr[0:64, 200:212], MAX))
+    vdo(V.tensor_tensor(tr[0:64, 224:230], tr[0:64, 212:218], tr[0:64, 218:224], MAX))
+    vdo(V.tensor_tensor(tr[0:64, 232:235], tr[0:64, 224:227], tr[0:64, 227:230], MAX))
+    vdo(V.tensor_tensor(tr[0:64, 236:237], tr[0:64, 232:233], tr[0:64, 233:234], MAX))
+    mcol = tr[0:64, 240:241]
+    n_mcol = vdo(V.tensor_tensor(mcol, tr[0:64, 236:237], tr[0:64, 234:235], MAX))
 
     PE.wait_ge(S.vq, n_mcol)
     PE.matmul(T.pT2[0:1, 0:64], mcol, T.idI[0:64, 0:64], True, True).then_inc(S.pt2, 1)
     V.wait_ge(S.pt2, 1)
     n_mrow = vdo(V.tensor_copy(T.mrow[0:1, :], T.pT2[0:1, 0:64]))
-    SC.wait_ge(S.vq, n_mrow)
-    SC.dma_start(T.m[:, :], T.mrow[0:1, :]).then_inc(S.outm, 16)
+    if is_rank:
+        SC.wait_ge(S.vq, n_mrow)
+        SC.dma_start(T.m[:, :], T.mrow[0:1, :]).then_inc(S.outm, 16)
 
-    PE.wait_ge(S.ini, nini)
     PE.wait_ge(S.vq, n_mrow)
-    PE.matmul(T.zB0[:, 0:64], T.nh[0:1, :], T.mrow[0:1, :], False, True).then_inc(S.pb0, 1)
-    PE.matmul(T.zB1[:, 0:64], T.nh[0:1, :], T.mrow[0:1, :], False, True).then_inc(S.pb1, 1)
-    V.wait_ge(S.pb0, 1)
-    n_r0 = vdo(V.tensor_tensor(T.R[:, 0:64], T.zB0[:, 0:64], T.zeros[:, :], MAX))
-    V.wait_ge(S.pb1, 1)
-    n_r1 = vdo(V.tensor_tensor(T.R[:, 64:128], T.zB1[:, 0:64], T.zeros[:, :], MAX))
+    PE.matmul(T.zB[:, 0:64], T.nh[0:1, :], T.mrow[0:1, :], False, True).then_inc(S.pb, 1)
+    V.wait_ge(S.pb, 1)
+    n_r = vdo(V.tensor_tensor(T.R[:, :], T.zB[:, 0:64], T.zeros[:, :], MAX))
+    PE.wait_ge(S.vq, n_r)
+    PE.matmul(T.pS[0:1, 0:64], T.ones[:, 0:1], T.R[:, :], True, True).then_inc(S.ps, 1)
+    V.wait_ge(S.ps, 1)
+    n_s = vdo(V.tensor_copy(T.srow[0:1, 0:TK], T.pS[0:1, 0:64]))
 
-    if R2_DRAM:
-        PE.wait_ge(S.vq, n_r0)
-        PE.matmul(T.pS[0:1, 0:64], T.ones[:, 0:1], T.R[:, 0:64], True, False)
-        PE.wait_ge(S.vq, n_r1)
-        PE.matmul(T.pS[0:1, 0:64], T.ones[:, 0:1], T.R[:, 64:128], False, True).then_inc(S.ps, 1)
-        V.wait_ge(S.ps, 1)
-        n_s = vdo(V.tensor_copy(T.srow[0:1, 0:TK], T.pS[0:1, 0:64]))
-        SY.wait_ge(S.vq, n_s)
-        SY.dma_start(T.land2[rank, :, 0], T.srow[0:1, :]).then_inc(S.st2, 16)
-        g.wait_ge(S.st2, 16)
-        send(T.land2[rank], S.arr2, one_each)
-        sent += NENG
-        SY.wait_ge(S.st2, 16)
-        SY.wait_ge(S.arr2, N - 1)
-        SY.dma_start(T.U2[0:N, 0:64], T.land2[:, 0:64, 0]).then_inc(S.u2, 16)
+    slot = r if is_rank else N + r
+    SY.wait_ge(S.vq, n_s)
+    SY.dma_start(T.land2[slot, :, 0], T.srow[0:1, :]).then_inc(S.st2, 16)
+    g.wait_ge(S.st2, 16)
+    send(T.land2[slot], S.arr2, readers2)
+    SY.wait_ge(S.st2, 16)
+
+    if is_rank:
+        SY.wait_ge(S.arr2, 2 * N - 1)
+        SY.dma_start(T.U2[0:2 * N, 0:64], T.land2[:, 0:64, 0]).then_inc(S.u2, 16)
         PE.wait_ge(S.u2, 16)
-        PE.matmul(T.pF[0:1, 0:64], T.ones[0:N, 0:1], T.U2[0:N, 0:64], True, True).then_inc(S.pf, 1)
+        PE.matmul(T.pF[0:1, 0:64], T.ones[0:2 * N, 0:1], T.U2[0:2 * N, 0:64], True, True).then_inc(S.pf, 1)
         V.wait_ge(S.pf, 1)
         n_f = vdo(V.tensor_copy(T.fin[0:1, :], T.pF[0:1, 0:64]))
         SY.wait_ge(S.vq, n_f)
         SY.dma_start(T.s[:, :], T.fin[0:1, :]).then_inc(S.outs, 16)
-    else:
-        PE.wait_ge(S.vq, n_r0)
-        PE.matmul(T.pS[0:64, 0:1], T.R[:, 0:64], T.ones[:, 0:1], True, False)
-        PE.wait_ge(S.vq, n_r1)
-        PE.matmul(T.pS[0:64, 0:1], T.R[:, 64:128], T.ones[:, 0:1], False, True).then_inc(S.ps, 1)
-        V.wait_ge(S.ps, 1)
-        n_s = vdo(V.tensor_copy(T.l2s[0:64, own], T.pS[0:64, 0:1]))
-        g.wait_ge(S.ini, nini)
-        g.wait_ge(S.vq, n_s)
-        send(T.l2s[:, own], S.arr2, all_bits)
-        sent += len(bits)
-        V.wait_ge(S.arr2, (N - 1) * len(bits))
-        n_f = fold12(ADD, T.l2s[0:64, 0:24:4], T.l2s[0:64, 24:48:4], 424, tr[0:64, 440:441])
-        SY.wait_ge(S.vq, n_f)
-        SY.dma_start(T.s[0, :], tr[0:64, 440:441]).then_inc(S.outs, 16)
-
-    SY.wait_ge(S.outs, 16)
-    SC.wait_ge(S.outm, 16)
-    g.wait_ge(S.sent, sent)
+        SY.wait_ge(S.outs, 16)
+        SC.wait_ge(S.outm, 16)
+    g.wait_ge(S.sent, 3 * NENG if is_rank else 2 * NENG)

@@ -1,35 +1,29 @@
 from concourse.bass import DstId, RemoteDMATransfer
-from concourse.mybir import AluOpType
+from concourse.mybir import AluOpType, AxisListType, ActivationFunctionType
 
 N, TK = 12, 64
 NCORES = 256
-NENG = 4
 
 SCRATCH = {
-    "wh": ("sbuf", [128, 448], "bfloat16"),
-    "zA": ("psum", [128, 512], "float32"),
-    "zB": ("psum", [128, 512], "float32"),
-    "pT1": ("psum", [128, 512], "float32"),
-    "pT2": ("psum", [128, 512], "float32"),
-    "pS": ("psum", [128, 512], "float32"),
+    "wh": ("sbuf", [128, 320], "bfloat16"),
+    "z": ("psum", [128, 512], "float32"),
+    "pT": ("psum", [128, 512], "float32"),
     "pF": ("psum", [128, 512], "float32"),
-    "tr": ("sbuf", [128, 256], "float32"),
+    "idI": ("sbuf", [128, 2 * N], "float32"),
     "ones": ("sbuf", [128, 4], "float32"),
-    "nh": ("sbuf", [128, 128], "float32"),
     "zeros": ("sbuf", [128, TK], "float32"),
-    "idA": ("sbuf", [128, TK + 1], "float32"),
-    "idD": ("dram", [1, TK * (TK + 1)], "float32"),
-    "idI": ("sbuf", [128, TK], "float32"),
-    "R": ("sbuf", [128, TK], "float32"),
+    "lm": ("sbuf", [128, 4], "float32"),
+    "nb": ("sbuf", [128, 4], "float32"),
+    "mcol": ("sbuf", [128, 4], "float32"),
+    "sp": ("sbuf", [128, 4], "float32"),
+    "relu": ("sbuf", [128, 128], "float32"),
     "U1": ("sbuf", [128, TK], "float32"),
     "U2": ("sbuf", [128, TK], "float32"),
-    "mrow": ("sbuf", [128, TK], "float32"),
-    "srow": ("sbuf", [128, 2 * TK], "float32"),
     "fin": ("sbuf", [128, TK], "float32"),
     "land1": ("dram", [N, 128, 1], "float32"),
     "land2": ("dram", [2 * N, 128, 1], "float32"),
 }
-SEMAPHORES = ["ld", "ini", "ida", "idd", "idr", "whr", "vq", "pza", "pt1", "pt2", "pb", "ps", "pf",
+SEMAPHORES = ["ld", "ini", "zf", "idd", "idr", "whr", "pz", "vl", "pt", "vb", "vm", "ac", "pf", "vf",
               "st1", "st2", "u1", "u2", "arr1", "arr2", "sent", "outm", "outs"]
 
 
@@ -48,9 +42,10 @@ def rank_program(g, core, T, topo):
     partner = helpers[r] if is_rank else ranks[r]
     S = T.sem
     V, PE, SY, SC = g.vector, g.tensor, g.sync, g.scalar
-    MAX = AluOpType.max
-    tr, wh = T.tr, T.wh
-    hS = wh[:, 320:384]
+    MAX, X = AluOpType.max, AxisListType.X
+    wh = T.wh
+    hS = wh[:, 256:320]
+    slot = r if is_rank else N + r
 
     def far_first(ds):
         return sorted(ds, key=lambda d: 0 if (topo.chip(d) != topo.chip(core) or topo.host(d) != topo.host(core))
@@ -61,8 +56,8 @@ def rank_program(g, core, T, topo):
     common = topo.mask(core, readers1[0])
     for d in readers1:
         common &= topo.mask(core, d)
-    bits = [1 << b for b in range(common.bit_length()) if (common >> b) & 1]
-    engines = bits[::len(bits) // NENG][:NENG]
+    engines = [1 << b for b in range(common.bit_length()) if (common >> b) & 1]
+    neng = len(engines)
 
     def dst_id(d):
         rid, pid = topo.addr(d, core)
@@ -70,8 +65,8 @@ def rank_program(g, core, T, topo):
 
     def send(ap, sem, readers):
         trs = []
-        for i in range(NENG):
-            ds = readers[i::NENG]
+        for i in range(neng):
+            ds = readers[i::neng]
             trs.append(RemoteDMATransfer(dst_ids=[dst_id(d) for d in ds], dma_engine_mask=engines[i], remote_sem=sem,
                                          srcs=[ap], dsts=[ap for _ in ds], alu_op=0))
         g.remote_dma_fused(trs, local_sem=S.sent)
@@ -80,105 +75,79 @@ def rank_program(g, core, T, topo):
         g.remote_dma_fused([RemoteDMATransfer(dst_ids=[dst_id(partner)], dma_engine_mask=sum(engines), remote_sem=sem,
                                               srcs=[ap], dsts=[ap], alu_op=0)], local_sem=S.sent)
 
-    vc = [0]
-
-    def vdo(ins):
-        ins.then_inc(S.vq, 1)
-        vc[0] += 1
-        V.wait_ge(S.vq, vc[0])
-        return vc[0]
-
-    fills = [(T.ones[:, 0:4], 1.0), (T.nh[0:1, :], -0.5), (T.zeros[:, :], 0.0), (T.srow[0:1, TK:2 * TK], 0.0)]
     if is_rank:
         SY.dma_start(wh[:, 0:256], T.w[:, :]).then_inc(S.ld, 16)
         SC.dma_start(hS, T.h[:, :]).then_inc(S.ld, 16)
-        fills = [(wh[:, 256:320], 0.0), (wh[:, 384:448], 0.0)] + fills
+        fills = [(T.zeros[:, :], 0.0), (T.ones[:, 0:4], 1.0)]
     else:
-        fills = [(T.idA[0:64, 1:TK + 1], 0.0), (T.idA[0:64, 0:1], 1.0), (T.idI[64:128, :], 0.0)] + fills
+        fills = [(T.idI[:, 0:N], 0.5), (T.idI[:, N:2 * N], 1.0), (T.zeros[:, :], 0.0)]
     for ap, c in fills:
         V.memset(ap, c).then_inc(S.ini, 1)
     nini = len(fills)
-    for q in (V, SY, SC, PE, g):
+    for q in (SC, PE, g):
         q.wait_ge(S.ini, nini)
+
+    nzf = 16
+    SC.dma_start(T.land2[slot, 64:128, 0], T.zeros[0:1, 0:64]).then_inc(S.zf, 16)
+    if is_rank:
+        SC.dma_start(T.land1[r, 64:128, 0], T.zeros[0:1, 0:64]).then_inc(S.zf, 16)
+        nzf = 32
 
     if is_rank:
         g.wait_ge(S.ld, 32)
-        hand(wh[:, 128:384], S.whr)
+        hand(wh[:, 128:320], S.whr)
         PE.wait_ge(S.ld, 32)
-        PE.matmul(T.zA[:, 0:128], wh[:, 320:448], wh[:, 0:128], True, False)
-        PE.matmul(T.zA[:, 0:128], wh[:, 256:384], wh[:, 128:256], False, True).then_inc(S.pza, 1)
-        PE.matmul(T.zB[:, 0:64], wh[:, 0:128], hS, True, False)
-        V.wait_ge(S.pza, 1)
-        vdo(V.tensor_copy(tr[:, 0:64], T.zA[:, 0:64]))
-        vdo(V.tensor_tensor(tr[:, 64:128], T.zA[:, 64:128], tr[:, 0:64], MAX))
-        lo, w, nxt = 64, 64, 128
-        while w > 1:
-            hw = w // 2
-            n_col = vdo(V.tensor_tensor(tr[:, nxt:nxt + hw], tr[:, lo:lo + hw], tr[:, lo + hw:lo + w], MAX))
-            lo, w, nxt = nxt, hw, nxt + max(hw, 4)
-        SY.wait_ge(S.vq, n_col)
-        SY.dma_start(T.land1[r, :, 0], tr[:, lo:lo + 1]).then_inc(S.st1, 16)
+        PE.matmul(T.z[0:64, 0:256], hS, wh[:, 0:256], True, True).then_inc(S.pz, 1)
+        V.wait_ge(S.pz, 1)
+        V.tensor_reduce(T.lm[0:64, 0:1], T.z[0:64, 0:256], X, MAX).then_inc(S.vl, 1)
+        SY.wait_ge(S.vl, 1)
+        SY.dma_start(T.land1[r, 0:64, 0], T.lm[0:64, 0:1]).then_inc(S.st1, 16)
+        g.wait_ge(S.zf, nzf)
         g.wait_ge(S.st1, 16)
         send(T.land1[r], S.arr1, readers1)
         SY.wait_ge(S.st1, 16)
         SY.wait_ge(S.arr1, N - 1)
-        PE.wait_ge(S.idr, NENG)
+        PE.wait_ge(S.idr, neng)
     else:
-        SC.dma_start(T.idD[0, :], T.idA[0:TK, 0:TK + 1]).then_inc(S.ida, 16)
-        SC.wait_ge(S.ida, 16)
-        SC.dma_start(T.idI[0:TK, 0:TK], T.idD[0, 0:TK * TK]).then_inc(S.idd, 16)
-        g.wait_ge(S.idd, 16)
+        g.affine_select(T.idI[:, :], T.idI[:, :], [[0, 2], [-1, N]], AluOpType.is_equal, 0.0, 0, 1).then_inc(S.idd, 1)
+        g.wait_ge(S.idd, 1)
         hand(T.idI[:, :], S.idr)
-        PE.wait_ge(S.whr, NENG)
-        PE.matmul(T.zB[:, 0:64], wh[:, 128:256], hS, True, False)
+        PE.wait_ge(S.whr, neng)
+        PE.matmul(T.z[0:64, 0:128], hS, wh[:, 128:256], True, True).then_inc(S.pz, 1)
         SY.wait_ge(S.arr1, N)
-        PE.wait_ge(S.idd, 16)
+        PE.wait_ge(S.idd, 1)
+        g.wait_ge(S.zf, nzf)
 
-    SY.dma_start(T.U1[0:2 * N, 0:64], T.land1[:, :, 0]).then_inc(S.u1, 16)
+    SY.dma_start(T.U1[0:N, 0:64], T.land1[:, 0:64, 0]).then_inc(S.u1, 16)
     PE.wait_ge(S.u1, 16)
-    PE.matmul(T.pT1[0:64, 0:2 * N], T.U1[0:2 * N, 0:64], T.idI[0:2 * N, 0:2 * N], True, True).then_inc(S.pt1, 1)
-    V.wait_ge(S.pt1, 1)
-    vdo(V.tensor_copy(tr[0:64, 200:212], T.pT1[0:64, 0:12]))
-    vdo(V.tensor_tensor(tr[0:64, 212:224], T.pT1[0:64, 12:24], tr[0:64, 200:212], MAX))
-    vdo(V.tensor_tensor(tr[0:64, 224:230], tr[0:64, 212:218], tr[0:64, 218:224], MAX))
-    vdo(V.tensor_tensor(tr[0:64, 232:235], tr[0:64, 224:227], tr[0:64, 227:230], MAX))
-    vdo(V.tensor_tensor(tr[0:64, 236:237], tr[0:64, 232:233], tr[0:64, 233:234], MAX))
-    mcol = tr[0:64, 240:241]
-    n_mcol = vdo(V.tensor_tensor(mcol, tr[0:64, 236:237], tr[0:64, 234:235], MAX))
-
-    PE.wait_ge(S.vq, n_mcol)
-    PE.matmul(T.pT2[0:1, 0:64], mcol, T.idI[0:64, 0:64], True, True).then_inc(S.pt2, 1)
-    V.wait_ge(S.pt2, 1)
-    n_mrow = vdo(V.tensor_copy(T.mrow[0:1, :], T.pT2[0:1, 0:64]))
+    PE.matmul(T.pT[0:64, 0:2 * N], T.U1[0:N, 0:64], T.idI[0:N, 0:2 * N], True, True).then_inc(S.pt, 1)
+    V.wait_ge(S.pt, 1)
+    V.tensor_reduce(T.nb[0:64, 0:1], T.pT[0:64, 0:N], X, MAX, negate=True).then_inc(S.vb, 1)
     if is_rank:
-        SC.wait_ge(S.vq, n_mrow)
-        SC.dma_start(T.m[:, :], T.mrow[0:1, :]).then_inc(S.outm, 16)
+        V.tensor_reduce(T.mcol[0:64, 0:1], T.pT[0:64, N:2 * N], X, MAX).then_inc(S.vm, 1)
 
-    PE.wait_ge(S.vq, n_mrow)
-    PE.matmul(T.zB[:, 0:64], T.nh[0:1, :], T.mrow[0:1, :], False, True).then_inc(S.pb, 1)
-    V.wait_ge(S.pb, 1)
-    n_r = vdo(V.tensor_tensor(T.R[:, :], T.zB[:, 0:64], T.zeros[:, :], MAX))
-    PE.wait_ge(S.vq, n_r)
-    PE.matmul(T.pS[0:1, 0:64], T.ones[:, 0:1], T.R[:, :], True, True).then_inc(S.ps, 1)
-    V.wait_ge(S.ps, 1)
-    n_s = vdo(V.tensor_copy(T.srow[0:1, 0:TK], T.pS[0:1, 0:64]))
+    SC.wait_ge(S.pz, 1)
+    SC.wait_ge(S.vb, 1)
+    SC.activation(T.relu[0:64, 0:128], T.z[0:64, 0:128], ActivationFunctionType.Relu, bias=T.nb[0:64, 0:1], scale=1.0,
+                  accum_out=T.sp[0:64, 0:1]).then_inc(S.ac, 1)
 
-    slot = r if is_rank else N + r
-    SY.wait_ge(S.vq, n_s)
-    SY.dma_start(T.land2[slot, :, 0], T.srow[0:1, :]).then_inc(S.st2, 16)
+    SC.wait_ge(S.ac, 1)
+    SC.dma_start(T.land2[slot, 0:64, 0], T.sp[0:64, 0:1]).then_inc(S.st2, 16)
     g.wait_ge(S.st2, 16)
     send(T.land2[slot], S.arr2, readers2)
-    SY.wait_ge(S.st2, 16)
 
     if is_rank:
+        SY.wait_ge(S.vm, 1)
+        SY.dma_start(T.m[0, :], T.mcol[0:64, 0:1]).then_inc(S.outm, 16)
+        SY.wait_ge(S.st2, 16)
         SY.wait_ge(S.arr2, 2 * N - 1)
         SY.dma_start(T.U2[0:2 * N, 0:64], T.land2[:, 0:64, 0]).then_inc(S.u2, 16)
         PE.wait_ge(S.u2, 16)
         PE.matmul(T.pF[0:1, 0:64], T.ones[0:2 * N, 0:1], T.U2[0:2 * N, 0:64], True, True).then_inc(S.pf, 1)
         V.wait_ge(S.pf, 1)
-        n_f = vdo(V.tensor_copy(T.fin[0:1, :], T.pF[0:1, 0:64]))
-        SY.wait_ge(S.vq, n_f)
+        V.tensor_copy(T.fin[0:1, :], T.pF[0:1, 0:64]).then_inc(S.vf, 1)
+        SY.wait_ge(S.vf, 1)
         SY.dma_start(T.s[:, :], T.fin[0:1, :]).then_inc(S.outs, 16)
         SY.wait_ge(S.outs, 16)
-        SC.wait_ge(S.outm, 16)
-    g.wait_ge(S.sent, 3 * NENG if is_rank else 2 * NENG)
+        SY.wait_ge(S.outm, 16)
+    g.wait_ge(S.sent, 3 * neng if is_rank else 2 * neng)

@@ -8,23 +8,19 @@ SCRATCH = {
     "wh": ("sbuf", [128, 320], "bfloat16"),
     "z": ("psum", [128, 512], "float32"),
     "pT": ("psum", [128, 512], "float32"),
-    "pF": ("psum", [128, 512], "float32"),
     "idI": ("sbuf", [128, 2 * N], "float32"),
-    "ones": ("sbuf", [128, 4], "float32"),
     "zeros": ("sbuf", [128, TK], "float32"),
     "lm": ("sbuf", [128, 4], "float32"),
     "nb": ("sbuf", [128, 4], "float32"),
     "mcol": ("sbuf", [128, 4], "float32"),
-    "sp": ("sbuf", [128, 4], "float32"),
-    "relu": ("sbuf", [128, 128], "float32"),
+    "scol": ("sbuf", [128, 4], "float32"),
+    "relu": ("sbuf", [128, 256], "float32"),
     "U1": ("sbuf", [128, TK], "float32"),
-    "U2": ("sbuf", [128, TK], "float32"),
-    "fin": ("sbuf", [128, TK], "float32"),
+    "L2": ("sbuf", [128, 4 * N], "float32"),
     "land1": ("dram", [N, 128, 1], "float32"),
-    "land2": ("dram", [2 * N, 128, 1], "float32"),
 }
-SEMAPHORES = ["ld", "ini", "zf", "idd", "idr", "whr", "pz", "vl", "pt", "vb", "vm", "ac", "pf", "vf",
-              "st1", "st2", "u1", "u2", "arr1", "arr2", "sent", "outm", "outs"]
+SEMAPHORES = ["ld", "ini", "zf", "idd", "idr", "whr", "pz", "vl", "pt", "vb", "vm", "ac", "vf",
+              "st1", "u1", "arr1", "arr2", "sent", "outm", "outs"]
 
 
 def rank_program(g, core, T, topo):
@@ -45,14 +41,15 @@ def rank_program(g, core, T, topo):
     MAX, X = AluOpType.max, AxisListType.X
     wh = T.wh
     hS = wh[:, 256:320]
-    slot = r if is_rank else N + r
+    mine = T.L2[:, 4 * r:4 * r + 4]
 
     def far_first(ds):
         return sorted(ds, key=lambda d: 0 if (topo.chip(d) != topo.chip(core) or topo.host(d) != topo.host(core))
                       and not (topo.mates(core, d) or topo.same_plane(core, d)) else 1)
 
     readers1 = far_first([d for d in ranks + helpers if d != core])
-    readers2 = far_first([d for d in ranks if d != core])
+    others = far_first([d for d in ranks if d != ranks[r]])
+    readers2 = others[1::2] if is_rank else others[0::2]
     common = topo.mask(core, readers1[0])
     for d in readers1:
         common &= topo.mask(core, d)
@@ -63,7 +60,7 @@ def rank_program(g, core, T, topo):
         rid, pid = topo.addr(d, core)
         return DstId(rid=rid, pnc=pid)
 
-    def send(ap, sem, readers):
+    def send_rows(ap, sem, readers):
         trs = []
         for i in range(neng):
             ds = readers[i::neng]
@@ -71,52 +68,47 @@ def rank_program(g, core, T, topo):
                                          srcs=[ap], dsts=[ap for _ in ds], alu_op=0))
         g.remote_dma_fused(trs, local_sem=S.sent)
 
-    def hand(ap, sem):
-        g.remote_dma_fused([RemoteDMATransfer(dst_ids=[dst_id(partner)], dma_engine_mask=sum(engines), remote_sem=sem,
-                                              srcs=[ap], dsts=[ap], alu_op=0)], local_sem=S.sent)
+    def send_block(ap, sem, readers):
+        g.remote_dma_fused([RemoteDMATransfer(dst_ids=[dst_id(d) for d in readers], dma_engine_mask=sum(engines),
+                                              remote_sem=sem, srcs=[ap], dsts=[ap for _ in readers], alu_op=0)],
+                           local_sem=S.sent)
 
     if is_rank:
         SY.dma_start(wh[:, 0:256], T.w[:, :]).then_inc(S.ld, 16)
         SC.dma_start(hS, T.h[:, :]).then_inc(S.ld, 16)
-        fills = [(T.zeros[:, :], 0.0), (T.ones[:, 0:4], 1.0)]
+        fills = [(T.zeros[:, :], 0.0), (mine, 0.0)]
     else:
-        fills = [(T.idI[:, 0:N], 0.5), (T.idI[:, N:2 * N], 1.0), (T.zeros[:, :], 0.0)]
+        fills = [(T.idI[:, 0:N], 0.5), (T.idI[:, N:2 * N], 1.0), (mine, 0.0)]
     for ap, c in fills:
         V.memset(ap, c).then_inc(S.ini, 1)
     nini = len(fills)
-    for q in (SC, PE, g):
+    for q in (SC, g):
         q.wait_ge(S.ini, nini)
 
-    nzf = 16
-    SC.dma_start(T.land2[slot, 64:128, 0], T.zeros[0:1, 0:64]).then_inc(S.zf, 16)
     if is_rank:
         SC.dma_start(T.land1[r, 64:128, 0], T.zeros[0:1, 0:64]).then_inc(S.zf, 16)
-        nzf = 32
-
-    if is_rank:
         g.wait_ge(S.ld, 32)
-        hand(wh[:, 128:320], S.whr)
+        send_block(wh[:, :], S.whr, [partner])
         PE.wait_ge(S.ld, 32)
         PE.matmul(T.z[0:64, 0:256], hS, wh[:, 0:256], True, True).then_inc(S.pz, 1)
         V.wait_ge(S.pz, 1)
         V.tensor_reduce(T.lm[0:64, 0:1], T.z[0:64, 0:256], X, MAX).then_inc(S.vl, 1)
         SY.wait_ge(S.vl, 1)
         SY.dma_start(T.land1[r, 0:64, 0], T.lm[0:64, 0:1]).then_inc(S.st1, 16)
-        g.wait_ge(S.zf, nzf)
+        g.wait_ge(S.zf, 16)
         g.wait_ge(S.st1, 16)
-        send(T.land1[r], S.arr1, readers1)
+        send_rows(T.land1[r], S.arr1, readers1)
         SY.wait_ge(S.st1, 16)
         SY.wait_ge(S.arr1, N - 1)
         PE.wait_ge(S.idr, neng)
     else:
         g.affine_select(T.idI[:, :], T.idI[:, :], [[0, 2], [-1, N]], AluOpType.is_equal, 0.0, 0, 1).then_inc(S.idd, 1)
         g.wait_ge(S.idd, 1)
-        hand(T.idI[:, :], S.idr)
+        send_block(T.idI[:, :], S.idr, [partner])
         PE.wait_ge(S.whr, neng)
-        PE.matmul(T.z[0:64, 0:128], hS, wh[:, 128:256], True, True).then_inc(S.pz, 1)
+        PE.matmul(T.z[0:64, 0:256], hS, wh[:, 0:256], True, True).then_inc(S.pz, 1)
         SY.wait_ge(S.arr1, N)
         PE.wait_ge(S.idd, 1)
-        g.wait_ge(S.zf, nzf)
 
     SY.dma_start(T.U1[0:N, 0:64], T.land1[:, 0:64, 0]).then_inc(S.u1, 16)
     PE.wait_ge(S.u1, 16)
@@ -128,26 +120,20 @@ def rank_program(g, core, T, topo):
 
     SC.wait_ge(S.pz, 1)
     SC.wait_ge(S.vb, 1)
-    SC.activation(T.relu[0:64, 0:128], T.z[0:64, 0:128], ActivationFunctionType.Relu, bias=T.nb[0:64, 0:1], scale=1.0,
-                  accum_out=T.sp[0:64, 0:1]).then_inc(S.ac, 1)
+    SC.activation(T.relu[0:64, 0:256], T.z[0:64, 0:256], ActivationFunctionType.Relu, bias=T.nb[0:64, 0:1], scale=1.0,
+                  accum_out=T.L2[0:64, 4 * r:4 * r + 1]).then_inc(S.ac, 1)
 
-    SC.wait_ge(S.ac, 1)
-    SC.dma_start(T.land2[slot, 0:64, 0], T.sp[0:64, 0:1]).then_inc(S.st2, 16)
-    g.wait_ge(S.st2, 16)
-    send(T.land2[slot], S.arr2, readers2)
+    g.wait_ge(S.ac, 1)
+    send_block(mine, S.arr2, readers2)
 
     if is_rank:
         SY.wait_ge(S.vm, 1)
         SY.dma_start(T.m[0, :], T.mcol[0:64, 0:1]).then_inc(S.outm, 16)
-        SY.wait_ge(S.st2, 16)
-        SY.wait_ge(S.arr2, 2 * N - 1)
-        SY.dma_start(T.U2[0:2 * N, 0:64], T.land2[:, 0:64, 0]).then_inc(S.u2, 16)
-        PE.wait_ge(S.u2, 16)
-        PE.matmul(T.pF[0:1, 0:64], T.ones[0:2 * N, 0:1], T.U2[0:2 * N, 0:64], True, True).then_inc(S.pf, 1)
-        V.wait_ge(S.pf, 1)
-        V.tensor_copy(T.fin[0:1, :], T.pF[0:1, 0:64]).then_inc(S.vf, 1)
+        V.wait_ge(S.ac, 1)
+        V.wait_ge(S.arr2, (N - 1) * neng)
+        V.tensor_reduce(T.scol[0:64, 0:1], T.L2[0:64, :], X, AluOpType.add).then_inc(S.vf, 1)
         SY.wait_ge(S.vf, 1)
-        SY.dma_start(T.s[:, :], T.fin[0:1, :]).then_inc(S.outs, 16)
+        SY.dma_start(T.s[0, :], T.scol[0:64, 0:1]).then_inc(S.outs, 16)
         SY.wait_ge(S.outs, 16)
         SY.wait_ge(S.outm, 16)
     g.wait_ge(S.sent, 3 * neng if is_rank else 2 * neng)

from concourse.bass import DstId, RemoteDMATransfer
from concourse.mybir import AluOpType, AxisListType, ActivationFunctionType

N, TK = 12, 64
NCORES = 256

SCRATCH = {
    "wh": ("sbuf", [128, 320], "bfloat16"),
    "z": ("psum", [128, 512], "float32"),
    "pT": ("psum", [128, 512], "float32"),
    "idI": ("sbuf", [128, 2 * N], "float32"),
    "zeros": ("sbuf", [128, TK], "float32"),
    "lm": ("sbuf", [128, 4], "float32"),
    "nb": ("sbuf", [128, 4], "float32"),
    "mcol": ("sbuf", [128, 4], "float32"),
    "scol": ("sbuf", [128, 4], "float32"),
    "relu": ("sbuf", [128, 256], "float32"),
    "U1": ("sbuf", [128, TK], "float32"),
    "L2": ("sbuf", [128, 4 * N], "float32"),
    "land1": ("dram", [N, 128, 1], "float32"),
}
SEMAPHORES = ["ld", "ini", "zf", "idd", "idr", "whr", "pz", "vl", "pt", "vb", "vm", "ac", "vf",
              "st1", "u1", "arr1", "arr2", "sent", "outm", "outs"]


def rank_program(g, core, T, topo):
    ranks = list(T.cores)
    helpers = []
    for rk in ranks:
        cand = [c for c in range(NCORES) if c != rk and topo.host(c) == topo.host(rk) and topo.chip(c) == topo.chip(rk)
                and all(topo.may_write(c, d) for d in ranks)]
        cand.sort(key=lambda c: 0 if topo.die(c) == topo.die(rk) else 1)
        helpers.append(cand[0])
    is_rank = core in ranks
    if not is_rank and core not in helpers:
        return
    r = ranks.index(core) if is_rank else helpers.index(core)
    partner = helpers[r] if is_rank else ranks[r]
    S = T.sem
    V, PE, SY, SC = g.vector, g.tensor, g.sync, g.scalar
    MAX, X = AluOpType.max, AxisListType.X
    wh = T.wh
    hS = wh[:, 256:320]
    mine = T.L2[:, 4 * r:4 * r + 4]

    def far_first(ds):
        return sorted(ds, key=lambda d: 0 if (topo.chip(d) != topo.chip(core) or topo.host(d) != topo.host(core))
                      and not (topo.mates(core, d) or topo.same_plane(core, d)) else 1)

    readers1 = far_first([d for d in ranks + helpers if d != core])
    others = far_first([d for d in ranks if d != ranks[r]])
    readers2 = others[1::2] if is_rank else others[0::2]
    common = topo.mask(core, readers1[0])
    for d in readers1:
        common &= topo.mask(core, d)
    engines = [1 << b for b in range(common.bit_length()) if (common >> b) & 1]
    neng = len(engines)

    def dst_id(d):
        rid, pid = topo.addr(d, core)
        return DstId(rid=rid, pnc=pid)

    def send_rows(ap, sem, readers):
        trs = []
        for i in range(neng):
            ds = readers[i::neng]
            trs.append(RemoteDMATransfer(dst_ids=[dst_id(d) for d in ds], dma_engine_mask=engines[i], remote_sem=sem,
                                         srcs=[ap], dsts=[ap for _ in ds], alu_op=0))
        g.remote_dma_fused(trs, local_sem=S.sent)

    def send_block(ap, sem, readers):
        g.remote_dma_fused([RemoteDMATransfer(dst_ids=[dst_id(d) for d in readers], dma_engine_mask=sum(engines),
                                              remote_sem=sem, srcs=[ap], dsts=[ap for _ in readers], alu_op=0)],
                           local_sem=S.sent)

    if is_rank:
        SY.dma_start(wh[:, 0:256], T.w[:, :]).then_inc(S.ld, 16)
        SC.dma_start(hS, T.h[:, :]).then_inc(S.ld, 16)
        fills = [(T.zeros[:, :], 0.0), (mine, 0.0)]
    else:
        fills = [(T.idI[:, 0:N], 0.5), (T.idI[:, N:2 * N], 1.0), (mine, 0.0)]
    for ap, c in fills:
        V.memset(ap, c).then_inc(S.ini, 1)
    nini = len(fills)
    for q in (SC, g):
        q.wait_ge(S.ini, nini)

    if is_rank:
        SC.dma_start(T.land1[r, 64:128, 0], T.zeros[0:1, 0:64]).then_inc(S.zf, 16)
        g.wait_ge(S.ld, 32)
        send_block(wh[:, :], S.whr, [partner])
        PE.wait_ge(S.ld, 32)
        PE.matmul(T.z[0:64, 0:256], hS, wh[:, 0:256], True, True).then_inc(S.pz, 1)
        V.wait_ge(S.pz, 1)
        V.tensor_reduce(T.lm[0:64, 0:1], T.z[0:64, 0:256], X, MAX).then_inc(S.vl, 1)
        SY.wait_ge(S.vl, 1)
        SY.dma_start(T.land1[r, 0:64, 0], T.lm[0:64, 0:1]).then_inc(S.st1, 16)
        g.wait_ge(S.zf, 16)
        g.wait_ge(S.st1, 16)
        send_rows(T.land1[r], S.arr1, readers1)
        SY.wait_ge(S.st1, 16)
        SY.wait_ge(S.arr1, N - 1)
        PE.wait_ge(S.idr, neng)
    else:
        g.affine_select(T.idI[:, :], T.idI[:, :], [[0, 2], [-1, N]], AluOpType.is_equal, 0.0, 0, 1).then_inc(S.idd, 1)
        g.wait_ge(S.idd, 1)
        send_block(T.idI[:, :], S.idr, [partner])
        PE.wait_ge(S.whr, neng)
        PE.matmul(T.z[0:64, 0:256], hS, wh[:, 0:256], True, True).then_inc(S.pz, 1)
        SY.wait_ge(S.arr1, N)
        PE.wait_ge(S.idd, 1)

    SY.dma_start(T.U1[0:N, 0:64], T.land1[:, 0:64, 0]).then_inc(S.u1, 16)
    PE.wait_ge(S.u1, 16)
    PE.matmul(T.pT[0:64, 0:2 * N], T.U1[0:N, 0:64], T.idI[0:N, 0:2 * N], True, True).then_inc(S.pt, 1)
    V.wait_ge(S.pt, 1)
    V.tensor_reduce(T.nb[0:64, 0:1], T.pT[0:64, 0:N], X, MAX, negate=True).then_inc(S.vb, 1)
    if is_rank:
        V.tensor_reduce(T.mcol[0:64, 0:1], T.pT[0:64, N:2 * N], X, MAX).then_inc(S.vm, 1)

    SC.wait_ge(S.pz, 1)
    SC.wait_ge(S.vb, 1)
    SC.activation(T.relu[0:64, 0:256], T.z[0:64, 0:256], ActivationFunctionType.Relu, bias=T.nb[0:64, 0:1], scale=1.0,
                  accum_out=T.L2[0:64, 4 * r:4 * r + 1]).then_inc(S.ac, 1)

    g.wait_ge(S.ac, 1)
    send_block(mine, S.arr2, readers2)

    if is_rank:
        SY.wait_ge(S.vm, 1)
        SY.dma_start(T.m[0, :], T.mcol[0:64, 0:1]).then_inc(S.outm, 16)
        V.wait_ge(S.ac, 1)
        V.wait_ge(S.arr2, (N - 1) * neng)
        V.tensor_reduce(T.scol[0:64, 0:1], T.L2[0:64, :], X, AluOpType.add).then_inc(S.vf, 1)
        SY.wait_ge(S.vf, 1)
        SY.dma_start(T.s[0, :], T.scol[0:64, 0:1]).then_inc(S.outs, 16)
        SY.wait_ge(S.outs, 16)
        SY.wait_ge(S.outm, 16)
    g.wait_ge(S.sent, 3 * neng if is_rank else 2 * neng)
